import numpy as np
import ml_dtypes


def mxq(x, axis, fmt="e4m3"):
    dtype, down = {"e4m3": (ml_dtypes.float8_e4m3fn, 7), "e5m2": (ml_dtypes.float8_e5m2, 14)}[fmt]
    v = np.moveaxis(np.asarray(x, np.float32).astype(ml_dtypes.bfloat16).astype(np.float64), axis, -1)
    blocks = v.reshape(v.shape[:-1] + (-1, 32))
    amax = np.abs(blocks).max(-1, keepdims=True)
    byte = np.maximum(np.where(amax > 0, np.frexp(amax)[1] - 1 + 127, 0) - down, 1)
    scale = np.exp2(byte - 127.0)
    codes = (blocks / scale).astype(np.float32).astype(dtype).astype(np.float64)
    return np.moveaxis((codes * scale).reshape(v.shape), -1, axis)


WIDE = False


def mx_kscale(k):
    if not WIDE:
        return np.ones(k)
    levels = np.array([30, -30])
    if k % 512:
        return np.exp2(np.random.permutation(np.resize(levels, k // 32))).repeat(32)
    a = np.empty((k // 512, 16))
    for p in range(k // 512):
        a[p, :8] = np.random.permutation(np.resize(levels, 8))
        for g in range(8):
            far = levels[np.abs(levels - a[p, g]) >= 10]
            a[p, g + 8] = far[np.random.randint(len(far))]
    return np.exp2(a.ravel()).repeat(32)


def f64(x):
    return np.asarray(x).astype(np.float64)


T, D, H = 2048, 1280, 512


def setup_inputs():
    n = np.random.standard_normal
    s1 = mx_kscale(T)[:, None]
    s2 = mx_kscale(T)[:, None]
    m = np.exp(0.5 * n((T, 1)))
    return {
        "x": (n((T, D)) * s1).astype(np.float32),
        "de": (m * n((T, H)) / np.sqrt(T) / s1).astype(np.float32),
        "dr": (m * n((T, D)) / np.sqrt(T) * s2).astype(np.float32),
        "e": (n((T, H)) / s2).astype(np.float32),
        "mom": (n((1280, 512))).astype(np.float32),
    }


def reference(x, de, dr, e, mom):
    x_ = mxq(f64(x), 0, "e4m3")
    de_ = mxq(f64(de), 0, "e5m2")
    dr_ = mxq(f64(dr), 0, "e5m2")
    e_ = mxq(f64(e), 0, "e4m3")
    y = x_.T @ de_ + dr_.T @ e_
    return 0.9 * f64(mom) + y

@@ -1,0 +1,185 @@
+from contextlib import ExitStack
+
+import concourse.mybir as mybir
+
+T, D, H = 2048, 1280, 512
+FLOPS = 2 * 2 * T * D * H
+DECAY = 0.9
+
+F32 = mybir.dt.float32
+BF16 = mybir.dt.bfloat16
+U32 = mybir.dt.uint32
+U8 = mybir.dt.uint8
+E4M3 = mybir.dt.float8_e4m3fn_x4
+E5M2 = mybir.dt.float8_e5m2_x4
+MULT = mybir.AluOpType.mult
+ADD = mybir.AluOpType.add
+
+P = 128
+PACK = 4
+ROWS = P * PACK
+PASSES = 2 * T // ROWS
+BANKS = 8
+GROUPS = ((0, 4), (4, 4), (8, 2))
+TILES = 10
+RUN = 4
+LAST_SPLIT = (256, 320)
+STORES = ((0, 2), (2, 2), (4, 2), (6, 2), (8, 1), (9, 1))
+
+
+def tile_mix_tied_ema_kernel(tc, x, de, dr, e, mom, out):
+    nc = tc.nc
+    last = PASSES - 1
+    wide_src = [(x, E4M3), (dr, E5M2)]
+    narrow_src = [(de, E5M2), (e, E4M3)]
+
+    def group_of(tile):
+        return [g for g, (first, n) in enumerate(GROUPS) if first <= tile < first + n][0]
+
+    def group_rows(dram, g):
+        first, n = GROUPS[g]
+        return dram[first * P : (first + n) * P, :].rearrange("(m i) h -> m i h", i=n)
+
+    with ExitStack() as ctx:
+        stage = ctx.enter_context(tc.tile_pool(name="stage", bufs=3))
+        half = ctx.enter_context(tc.tile_pool(name="half", bufs=2))
+        keep = ctx.enter_context(tc.tile_pool(name="keep", bufs=1))
+        psum = ctx.enter_context(tc.psum_pool(name="psum", bufs=1))
+        ctx.enter_context(tc.manual_schedule())
+
+        wide_codes = keep.tile([P, PASSES, D], U32, align_bytes=64)
+        wide_scales = keep.tile([P, PASSES, D], U8, align_bytes=64)
+        narrow_codes = keep.tile([P, PASSES, H], U32, align_bytes=64)
+        narrow_scales = keep.tile([P, PASSES, H], U8, align_bytes=64)
+        mom_sb = keep.tile([P, TILES, H], F32)
+        res = keep.tile([P, TILES, H], F32)
+        wide_raw, narrow_raw, wide_bf, narrow_bf, acc = {}, {}, {}, {}, {}
+
+        def pass_rows(dram, s):
+            t0 = (s // 2) * ROWS
+            return dram[t0 : t0 + ROWS, :].rearrange("(p j) w -> p j w", j=PACK)
+
+        def load_wide(s):
+            wide_raw[s] = stage.tile([P, PACK, D], F32, name="wide_raw")
+            nc.sync.dma_start(out=wide_raw[s][:], in_=pass_rows(wide_src[s % 2][0], s))
+
+        def load_narrow(s):
+            narrow_raw[s] = stage.tile([P, PACK, H], F32, name="narrow_raw")
+            nc.sync.dma_start(out=narrow_raw[s][:], in_=pass_rows(narrow_src[s % 2][0], s))
+
+        def cast_wide(copy, s, g, m0=0, m1=P):
+            first, n = GROUPS[g]
+            if m0 == 0:
+                pool = stage if g == 1 else half
+                wide_bf[s, g] = pool.tile([P, n, P, PACK], BF16, name="wide_bf%d" % g, align_bytes=64)
+            src = wide_raw[s][:, :, first * P + n * m0 : first * P + n * m1]
+            copy(
+                out=wide_bf[s, g][:, :, m0:m1, :].rearrange("p i m j -> p m j i"),
+                in_=src.rearrange("p j (m i) -> p m j i", i=n),
+            )
+
+        def cast_narrow(copy, s, c0=0, c1=H):
+            if c0 == 0:
+                narrow_bf[s] = half.tile([P, H, PACK], BF16, name="narrow_bf", align_bytes=64)
+            copy(
+                out=narrow_bf[s][:, c0:c1, :].rearrange("p (c i) j -> p c j i", i=RUN),
+                in_=narrow_raw[s][:, :, c0:c1].rearrange("p j (c i) -> p c j i", i=RUN),
+            )
+
+        def quantise_wide(s, g, i0=0, i1=None):
+            first, n = GROUPS[g]
+            i1 = n if i1 is None else i1
+            cols = slice((first + i0) * P, (first + i1) * P)
+            nc.vector.quantize_mx(
+                out=wide_codes[:, s, cols].bitcast(wide_src[s % 2][1]),
+                scales=wide_scales[:, s, cols],
+                in_=wide_bf[s, g][:, i0:i1, :, :].rearrange("p i m j -> p (i m j)"),
+            )
+
+        def quantise_narrow(s, c0=0, c1=H):
+            nc.vector.quantize_mx(
+                out=narrow_codes[:, s, c0:c1].bitcast(narrow_src[s % 2][1]),
+                scales=narrow_scales[:, s, c0:c1],
+                in_=narrow_bf[s][:, c0:c1, :].rearrange("p c j -> p (c j)"),
+            )
+
+        def multiply(s, tile):
+            if s == 0:
+                acc[tile] = psum.tile([P, H], F32, name="bank%d" % (tile % BANKS))
+            cols = slice(tile * P, (tile + 1) * P)
+            nc.tensor.matmul_mx(
+                out=acc[tile][:],
+                lhsT=wide_codes[:, s, cols].bitcast(wide_src[s % 2][1]),
+                lhsT_scale=wide_scales[:, s, cols],
+                rhs=narrow_codes[:, s, :].bitcast(narrow_src[s % 2][1]),
+                rhs_scale=narrow_scales[:, s, :],
+                start=(s == 0),
+                stop=(s == last),
+            )
+
+        def multiply_group(s, g):
+            first, n = GROUPS[g]
+            for tile in range(first, first + n):
+                multiply(s, tile)
+
+        def update(tile):
+            nc.vector.scalar_tensor_tensor(
+                out=res[:, tile, :], in0=mom_sb[:, tile, :], scalar=DECAY, in1=acc[tile][:], op0=MULT, op1=ADD
+            )
+            for first, n in STORES:
+                if first + n - 1 == tile:
+                    g = group_of(tile)
+                    i0 = first - GROUPS[g][0]
+                    nc.sync.dma_start(out=group_rows(out, g)[:, i0 : i0 + n, :], in_=res[:, first : first + n, :])
+
+        vcopy, scopy = nc.vector.tensor_copy, nc.scalar.copy
+
+        load_narrow(0)
+        load_wide(0)
+        load_narrow(1)
+        load_wide(1)
+        for s in range(last):
+            if s + 2 < last:
+                load_narrow(s + 2)
+                load_wide(s + 2)
+            elif s + 2 == last:
+                load_wide(last)
+                load_narrow(last)
+                for g, (first, n) in enumerate(GROUPS):
+                    nc.sync.dma_start(out=mom_sb[:, first : first + n, :], in_=group_rows(mom, g))
+            cast_narrow(scopy, s)
+            cast_wide(scopy, s, 1)
+            quantise_narrow(s)
+            cast_wide(vcopy, s, 0)
+            cast_wide(vcopy, s, 2)
+            quantise_wide(s, 0)
+            quantise_wide(s, 2)
+            multiply_group(s, 0)
+            if s < last - 1:
+                quantise_wide(s, 1)
+                multiply_group(s, 1)
+
+        cast_wide(scopy, last, 1)
+        cast_wide(vcopy, last, 0, 0, P // 2)
+        quantise_wide(last - 1, 1, 0, 2)
+        cast_wide(vcopy, last, 0, P // 2, P)
+        quantise_wide(last - 1, 1, 2, 4)
+        multiply_group(last - 1, 1)
+        quantise_wide(last, 0)
+        cast_narrow(vcopy, last, 0, LAST_SPLIT[0])
+        cast_narrow(vcopy, last, LAST_SPLIT[0], LAST_SPLIT[1])
+        cast_narrow(scopy, last, LAST_SPLIT[1], H)
+        cast_wide(scopy, last, 2)
+        quantise_narrow(last, 0, H // 2)
+        quantise_narrow(last, H // 2, H)
+        quantise_wide(last, 1)
+        multiply_group(last, 0)
+        multiply_group(last, 1)
+        update(0)
+        update(1)
+        quantise_wide(last, 2)
+        for tile in range(BANKS, TILES):
+            for s in range(PASSES):
+                multiply(s, tile)
+        for tile in range(2, TILES):
+            update(tile)

@@ -51,8 +51,8 @@ def tile_mix_tied_ema_kernel(tc, x, de, dr, e, mom, out):
         wide_scales = keep.tile([P, PASSES, D], U8, align_bytes=64)
         narrow_codes = keep.tile([P, PASSES, H], U32, align_bytes=64)
         narrow_scales = keep.tile([P, PASSES, H], U8, align_bytes=64)
-        mom_sb = keep.tile([P, TILES, H], F32)
-        res = keep.tile([P, TILES, H], F32)
+        mom_sb = keep.tile([P, TILES, H], F32, align_bytes=256)
+        res = keep.tile([P, TILES, H], F32, align_bytes=256)
         wide_raw, narrow_raw, wide_bf, narrow_bf, acc = {}, {}, {}, {}, {}
 
         def pass_rows(dram, s):
@@ -60,11 +60,11 @@ def tile_mix_tied_ema_kernel(tc, x, de, dr, e, mom, out):
             return dram[t0 : t0 + ROWS, :].rearrange("(p j) w -> p j w", j=PACK)
 
         def load_wide(s):
-            wide_raw[s] = stage.tile([P, PACK, D], F32, name="wide_raw")
+            wide_raw[s] = stage.tile([P, PACK, D], F32, name="wide_raw", align_bytes=256)
             nc.sync.dma_start(out=wide_raw[s][:], in_=pass_rows(wide_src[s % 2][0], s))
 
         def load_narrow(s):
-            narrow_raw[s] = stage.tile([P, PACK, H], F32, name="narrow_raw")
+            narrow_raw[s] = stage.tile([P, PACK, H], F32, name="narrow_raw", align_bytes=256)
             nc.sync.dma_start(out=narrow_raw[s][:], in_=pass_rows(narrow_src[s % 2][0], s))
 
         def cast_wide(copy, s, g, m0=0, m1=P):

@@ -52,7 +52,6 @@ def tile_mix_tied_ema_kernel(tc, x, de, dr, e, mom, out):
         narrow_codes = keep.tile([P, PASSES, H], U32, align_bytes=64)
         narrow_scales = keep.tile([P, PASSES, H], U8, align_bytes=64)
         mom_sb = keep.tile([P, TILES, H], F32, align_bytes=256)
-        res = keep.tile([P, TILES, H], F32, align_bytes=256)
         wide_raw, narrow_raw, wide_bf, narrow_bf, acc = {}, {}, {}, {}, {}
 
         def pass_rows(dram, s):
@@ -62,6 +61,13 @@ def tile_mix_tied_ema_kernel(tc, x, de, dr, e, mom, out):
         def load_wide(s):
             wide_raw[s] = stage.tile([P, PACK, D], F32, name="wide_raw", align_bytes=256)
             nc.sync.dma_start(out=wide_raw[s][:], in_=pass_rows(wide_src[s % 2][0], s))
+
+        def load_first_narrows():
+            both = keep.tile([P, 2, PACK, H], F32, align_bytes=256)
+            narrow_raw[0], narrow_raw[2] = both[:, 0], both[:, 1]
+            nc.sync.dma_start(
+                out=both[:], in_=de[0 : 2 * ROWS, :].rearrange("(g p j) w -> p g j w", g=2, j=PACK)
+            )
 
         def load_narrow(s):
             narrow_raw[s] = stage.tile([P, PACK, H], F32, name="narrow_raw", align_bytes=256)
@@ -124,23 +130,24 @@ def tile_mix_tied_ema_kernel(tc, x, de, dr, e, mom, out):
 
         def update(tile):
             nc.vector.scalar_tensor_tensor(
-                out=res[:, tile, :], in0=mom_sb[:, tile, :], scalar=DECAY, in1=acc[tile][:], op0=MULT, op1=ADD
+                out=mom_sb[:, tile, :], in0=mom_sb[:, tile, :], scalar=DECAY, in1=acc[tile][:], op0=MULT, op1=ADD
             )
             for first, n in STORES:
                 if first + n - 1 == tile:
                     g = group_of(tile)
                     i0 = first - GROUPS[g][0]
-                    nc.sync.dma_start(out=group_rows(out, g)[:, i0 : i0 + n, :], in_=res[:, first : first + n, :])
+                    nc.sync.dma_start(out=group_rows(out, g)[:, i0 : i0 + n, :], in_=mom_sb[:, first : first + n, :])
 
         vcopy, scopy = nc.vector.tensor_copy, nc.scalar.copy
 
-        load_narrow(0)
+        load_first_narrows()
         load_wide(0)
         load_narrow(1)
         load_wide(1)
         for s in range(last):
             if s + 2 < last:
-                load_narrow(s + 2)
+                if s > 0:
+                    load_narrow(s + 2)
                 load_wide(s + 2)
             elif s + 2 == last:
                 load_wide(last)

@@ -84,6 +84,16 @@ def tile_mix_tied_ema_kernel(tc, x, de, dr, e, mom, out):
                 in_=src.rearrange("p j (m i) -> p m j i", i=n),
             )
 
+        def cast_wide_tiles(copy, s, g, i0, i1):
+            first, n = GROUPS[g]
+            if i0 == 0:
+                wide_bf[s, g] = stage.tile([P, n, P, PACK], BF16, name="wide_bf%d" % g, align_bytes=64)
+            src = wide_raw[s][:, :, first * P : (first + n) * P]
+            copy(
+                out=wide_bf[s, g][:, i0:i1, :, :].rearrange("p i m j -> p m j i"),
+                in_=src.rearrange("p j (m i) -> p m j i", i=n)[:, :, :, i0:i1],
+            )
+
         def cast_narrow(copy, s, c0=0, c1=H):
             if c0 == 0:
                 narrow_bf[s] = half.tile([P, H, PACK], BF16, name="narrow_bf", align_bytes=64)
@@ -161,28 +171,39 @@ def tile_mix_tied_ema_kernel(tc, x, de, dr, e, mom, out):
             cast_wide(vcopy, s, 2)
             quantise_wide(s, 0)
             quantise_wide(s, 2)
-            multiply_group(s, 0)
+            if s < last - 1:
+                multiply_group(s, 0)
             if s < last - 1:
                 quantise_wide(s, 1)
+            if s < last - 2:
                 multiply_group(s, 1)
 
-        cast_wide(scopy, last, 1)
-        cast_wide(vcopy, last, 0, 0, P // 2)
         quantise_wide(last - 1, 1, 0, 2)
-        cast_wide(vcopy, last, 0, P // 2, P)
+        for tile in (4, 5):
+            multiply(last - 1, tile)
+        multiply_group(last - 2, 1)
+        for tile in (0, 1):
+            multiply(last - 1, tile)
+        cast_wide_tiles(scopy, last, 1, 0, 2)
+        cast_wide(vcopy, last, 0)
         quantise_wide(last - 1, 1, 2, 4)
-        multiply_group(last - 1, 1)
+        for tile in (6, 7, 2, 3):
+            multiply(last - 1, tile)
         quantise_wide(last, 0)
         cast_narrow(vcopy, last, 0, LAST_SPLIT[0])
         cast_narrow(vcopy, last, LAST_SPLIT[0], LAST_SPLIT[1])
         cast_narrow(scopy, last, LAST_SPLIT[1], H)
+        cast_wide_tiles(scopy, last, 1, 2, 4)
         cast_wide(scopy, last, 2)
         quantise_narrow(last, 0, H // 2)
         quantise_narrow(last, H // 2, H)
-        quantise_wide(last, 1)
-        multiply_group(last, 0)
-        multiply_group(last, 1)
+        quantise_wide(last, 1, 0, 2)
+        for tile in range(6):
+            multiply(last, tile)
         update(0)
+        quantise_wide(last, 1, 2, 4)
+        for tile in (6, 7):
+            multiply(last, tile)
         update(1)
         quantise_wide(last, 2)
         for tile in range(BANKS, TILES):

@@ -18,13 +18,14 @@ ADD = mybir.AluOpType.add
 P = 128
 PACK = 4
 ROWS = P * PACK
-PASSES = 2 * T // ROWS
+CHUNKS = T // ROWS
+PASSES = 2 * CHUNKS
 BANKS = 8
 GROUPS = ((0, 4), (4, 4), (8, 2))
 TILES = 10
 RUN = 4
 LAST_SPLIT = (256, 320)
-STORES = ((0, 2), (2, 2), (4, 2), (6, 2), (8, 1), (9, 1))
+STORES = ((0, 2), (2, 2), (4, 2), (6, 2), (8, 2))
 
 
 def tile_mix_tied_ema_kernel(tc, x, de, dr, e, mom, out):
@@ -41,7 +42,7 @@ def tile_mix_tied_ema_kernel(tc, x, de, dr, e, mom, out):
         return dram[first * P : (first + n) * P, :].rearrange("(m i) h -> m i h", i=n)
 
     with ExitStack() as ctx:
-        stage = ctx.enter_context(tc.tile_pool(name="stage", bufs=3))
+        stage = ctx.enter_context(tc.tile_pool(name="stage", bufs=2))
         half = ctx.enter_context(tc.tile_pool(name="half", bufs=2))
         keep = ctx.enter_context(tc.tile_pool(name="keep", bufs=1))
         psum = ctx.enter_context(tc.psum_pool(name="psum", bufs=1))
@@ -54,24 +55,24 @@ def tile_mix_tied_ema_kernel(tc, x, de, dr, e, mom, out):
         mom_sb = keep.tile([P, TILES, H], F32, align_bytes=256)
         wide_raw, narrow_raw, wide_bf, narrow_bf, acc = {}, {}, {}, {}, {}
 
-        def pass_rows(dram, s):
-            t0 = (s // 2) * ROWS
-            return dram[t0 : t0 + ROWS, :].rearrange("(p j) w -> p j w", j=PACK)
+        def rows(src, s, n):
+            t0 = (s % CHUNKS) * ROWS
+            return src[s // CHUNKS][0][t0 : t0 + n * ROWS, :].rearrange("(g p j) w -> p g j w", g=n, j=PACK)
 
-        def load_wide(s):
-            wide_raw[s] = stage.tile([P, PACK, D], F32, name="wide_raw", align_bytes=256)
-            nc.sync.dma_start(out=wide_raw[s][:], in_=pass_rows(wide_src[s % 2][0], s))
+        def load_wide(s, n):
+            if s % 2 == 0:
+                pair = stage.tile([P, 2, PACK, D], F32, name="wide_raw", align_bytes=256)
+                wide_raw[s], wide_raw[s + 1], wide_raw["pair"] = pair[:, 0], pair[:, 1], pair
+            nc.sync.dma_start(out=wide_raw["pair"][:, s % 2 : s % 2 + n], in_=rows(wide_src, s, n))
 
-        def load_first_narrows():
-            both = keep.tile([P, 2, PACK, H], F32, align_bytes=256)
-            narrow_raw[0], narrow_raw[2] = both[:, 0], both[:, 1]
-            nc.sync.dma_start(
-                out=both[:], in_=de[0 : 2 * ROWS, :].rearrange("(g p j) w -> p g j w", g=2, j=PACK)
-            )
-
-        def load_narrow(s):
-            narrow_raw[s] = stage.tile([P, PACK, H], F32, name="narrow_raw", align_bytes=256)
-            nc.sync.dma_start(out=narrow_raw[s][:], in_=pass_rows(narrow_src[s % 2][0], s))
+        def load_narrow(s, n):
+            if s % CHUNKS == 0:
+                whole = keep.tile([P, CHUNKS, PACK, H], F32, name="narrow_raw", align_bytes=256)
+                narrow_raw["whole"] = whole
+                for c in range(CHUNKS):
+                    narrow_raw[s + c] = whole[:, c]
+            c = s % CHUNKS
+            nc.sync.dma_start(out=narrow_raw["whole"][:, c : c + n], in_=rows(narrow_src, s, n))
 
         def cast_wide(copy, s, g, m0=0, m1=P):
             first, n = GROUPS[g]
@@ -107,14 +108,14 @@ def tile_mix_tied_ema_kernel(tc, x, de, dr, e, mom, out):
             i1 = n if i1 is None else i1
             cols = slice((first + i0) * P, (first + i1) * P)
             nc.vector.quantize_mx(
-                out=wide_codes[:, s, cols].bitcast(wide_src[s % 2][1]),
+                out=wide_codes[:, s, cols].bitcast(wide_src[s // CHUNKS][1]),
                 scales=wide_scales[:, s, cols],
                 in_=wide_bf[s, g][:, i0:i1, :, :].rearrange("p i m j -> p (i m j)"),
             )
 
         def quantise_narrow(s, c0=0, c1=H):
             nc.vector.quantize_mx(
-                out=narrow_codes[:, s, c0:c1].bitcast(narrow_src[s % 2][1]),
+                out=narrow_codes[:, s, c0:c1].bitcast(narrow_src[s // CHUNKS][1]),
                 scales=narrow_scales[:, s, c0:c1],
                 in_=narrow_bf[s][:, c0:c1, :].rearrange("p c j -> p (c j)"),
             )
@@ -125,9 +126,9 @@ def tile_mix_tied_ema_kernel(tc, x, de, dr, e, mom, out):
             cols = slice(tile * P, (tile + 1) * P)
             nc.tensor.matmul_mx(
                 out=acc[tile][:],
-                lhsT=wide_codes[:, s, cols].bitcast(wide_src[s % 2][1]),
+                lhsT=wide_codes[:, s, cols].bitcast(wide_src[s // CHUNKS][1]),
                 lhsT_scale=wide_scales[:, s, cols],
-                rhs=narrow_codes[:, s, :].bitcast(narrow_src[s % 2][1]),
+                rhs=narrow_codes[:, s, :].bitcast(narrow_src[s // CHUNKS][1]),
                 rhs_scale=narrow_scales[:, s, :],
                 start=(s == 0),
                 stop=(s == last),
@@ -150,23 +151,24 @@ def tile_mix_tied_ema_kernel(tc, x, de, dr, e, mom, out):
 
         vcopy, scopy = nc.vector.tensor_copy, nc.scalar.copy
 
-        load_first_narrows()
-        load_wide(0)
-        load_narrow(1)
-        load_wide(1)
+        load_narrow(0, CHUNKS)
+        load_wide(0, 2)
+        load_wide(2, 2)
         for s in range(last):
-            if s + 2 < last:
-                if s > 0:
-                    load_narrow(s + 2)
-                load_wide(s + 2)
-            elif s + 2 == last:
-                load_wide(last)
-                load_narrow(last)
+            if s % CHUNKS == 0:
+                for c in range(s, min(s + CHUNKS, last)):
+                    cast_narrow(scopy, c)
+                    quantise_narrow(c)
+            if s == 2:
+                load_narrow(CHUNKS, CHUNKS - 1)
+                load_wide(CHUNKS, 2)
+            if s == CHUNKS:
+                load_wide(last - 1, 1)
+                load_wide(last, 1)
+                load_narrow(last, 1)
                 for g, (first, n) in enumerate(GROUPS):
                     nc.sync.dma_start(out=mom_sb[:, first : first + n, :], in_=group_rows(mom, g))
-            cast_narrow(scopy, s)
             cast_wide(scopy, s, 1)
-            quantise_narrow(s)
             cast_wide(vcopy, s, 0)
             cast_wide(vcopy, s, 2)
             quantise_wide(s, 0)

from contextlib import ExitStack

import concourse.mybir as mybir

T, D, H = 2048, 1280, 512
FLOPS = 2 * 2 * T * D * H
DECAY = 0.9

F32 = mybir.dt.float32
BF16 = mybir.dt.bfloat16
U32 = mybir.dt.uint32
U8 = mybir.dt.uint8
E4M3 = mybir.dt.float8_e4m3fn_x4
E5M2 = mybir.dt.float8_e5m2_x4
MULT = mybir.AluOpType.mult
ADD = mybir.AluOpType.add

P = 128
PACK = 4
ROWS = P * PACK
CHUNKS = T // ROWS
PASSES = 2 * CHUNKS
BANKS = 8
GROUPS = ((0, 4), (4, 4), (8, 2))
TILES = 10
RUN = 4
LAST_SPLIT = (256, 320)
STORES = ((0, 2), (2, 2), (4, 2), (6, 2), (8, 2))


def tile_mix_tied_ema_kernel(tc, x, de, dr, e, mom, out):
    nc = tc.nc
    last = PASSES - 1
    wide_src = [(x, E4M3), (dr, E5M2)]
    narrow_src = [(de, E5M2), (e, E4M3)]

    def group_of(tile):
        return [g for g, (first, n) in enumerate(GROUPS) if first <= tile < first + n][0]

    def group_rows(dram, g):
        first, n = GROUPS[g]
        return dram[first * P : (first + n) * P, :].rearrange("(m i) h -> m i h", i=n)

    with ExitStack() as ctx:
        stage = ctx.enter_context(tc.tile_pool(name="stage", bufs=2))
        half = ctx.enter_context(tc.tile_pool(name="half", bufs=2))
        keep = ctx.enter_context(tc.tile_pool(name="keep", bufs=1))
        psum = ctx.enter_context(tc.psum_pool(name="psum", bufs=1))
        ctx.enter_context(tc.manual_schedule())

        wide_codes = keep.tile([P, PASSES, D], U32, align_bytes=64)
        wide_scales = keep.tile([P, PASSES, D], U8, align_bytes=64)
        narrow_codes = keep.tile([P, PASSES, H], U32, align_bytes=64)
        narrow_scales = keep.tile([P, PASSES, H], U8, align_bytes=64)
        mom_sb = keep.tile([P, TILES, H], F32, align_bytes=256)
        wide_raw, narrow_raw, wide_bf, narrow_bf, acc = {}, {}, {}, {}, {}

        def rows(src, s, n):
            t0 = (s % CHUNKS) * ROWS
            return src[s // CHUNKS][0][t0 : t0 + n * ROWS, :].rearrange("(g p j) w -> p g j w", g=n, j=PACK)

        def load_wide(s, n):
            if s % 2 == 0:
                pair = stage.tile([P, 2, PACK, D], F32, name="wide_raw", align_bytes=256)
                wide_raw[s], wide_raw[s + 1], wide_raw["pair"] = pair[:, 0], pair[:, 1], pair
            nc.sync.dma_start(out=wide_raw["pair"][:, s % 2 : s % 2 + n], in_=rows(wide_src, s, n))

        def load_narrow(s, n):
            if s % CHUNKS == 0:
                whole = keep.tile([P, CHUNKS, PACK, H], F32, name="narrow_raw", align_bytes=256)
                narrow_raw["whole"] = whole
                for c in range(CHUNKS):
                    narrow_raw[s + c] = whole[:, c]
            c = s % CHUNKS
            nc.sync.dma_start(out=narrow_raw["whole"][:, c : c + n], in_=rows(narrow_src, s, n))

        def cast_wide(copy, s, g, m0=0, m1=P):
            first, n = GROUPS[g]
            if m0 == 0:
                pool = stage if g == 1 else half
                wide_bf[s, g] = pool.tile([P, n, P, PACK], BF16, name="wide_bf%d" % g, align_bytes=64)
            src = wide_raw[s][:, :, first * P + n * m0 : first * P + n * m1]
            copy(
                out=wide_bf[s, g][:, :, m0:m1, :].rearrange("p i m j -> p m j i"),
                in_=src.rearrange("p j (m i) -> p m j i", i=n),
            )

        def cast_wide_tiles(copy, s, g, i0, i1):
            first, n = GROUPS[g]
            if i0 == 0:
                wide_bf[s, g] = stage.tile([P, n, P, PACK], BF16, name="wide_bf%d" % g, align_bytes=64)
            src = wide_raw[s][:, :, first * P : (first + n) * P]
            copy(
                out=wide_bf[s, g][:, i0:i1, :, :].rearrange("p i m j -> p m j i"),
                in_=src.rearrange("p j (m i) -> p m j i", i=n)[:, :, :, i0:i1],
            )

        def cast_narrow(copy, s, c0=0, c1=H):
            if c0 == 0:
                narrow_bf[s] = half.tile([P, H, PACK], BF16, name="narrow_bf", align_bytes=64)
            copy(
                out=narrow_bf[s][:, c0:c1, :].rearrange("p (c i) j -> p c j i", i=RUN),
                in_=narrow_raw[s][:, :, c0:c1].rearrange("p j (c i) -> p c j i", i=RUN),
            )

        def quantise_wide(s, g, i0=0, i1=None):
            first, n = GROUPS[g]
            i1 = n if i1 is None else i1
            cols = slice((first + i0) * P, (first + i1) * P)
            nc.vector.quantize_mx(
                out=wide_codes[:, s, cols].bitcast(wide_src[s // CHUNKS][1]),
                scales=wide_scales[:, s, cols],
                in_=wide_bf[s, g][:, i0:i1, :, :].rearrange("p i m j -> p (i m j)"),
            )

        def quantise_narrow(s, c0=0, c1=H):
            nc.vector.quantize_mx(
                out=narrow_codes[:, s, c0:c1].bitcast(narrow_src[s // CHUNKS][1]),
                scales=narrow_scales[:, s, c0:c1],
                in_=narrow_bf[s][:, c0:c1, :].rearrange("p c j -> p (c j)"),
            )

        def multiply(s, tile):
            if s == 0:
                acc[tile] = psum.tile([P, H], F32, name="bank%d" % (tile % BANKS))
            cols = slice(tile * P, (tile + 1) * P)
            nc.tensor.matmul_mx(
                out=acc[tile][:],
                lhsT=wide_codes[:, s, cols].bitcast(wide_src[s // CHUNKS][1]),
                lhsT_scale=wide_scales[:, s, cols],
                rhs=narrow_codes[:, s, :].bitcast(narrow_src[s // CHUNKS][1]),
                rhs_scale=narrow_scales[:, s, :],
                start=(s == 0),
                stop=(s == last),
            )

        def multiply_group(s, g):
            first, n = GROUPS[g]
            for tile in range(first, first + n):
                multiply(s, tile)

        def update(tile):
            nc.vector.scalar_tensor_tensor(
                out=mom_sb[:, tile, :], in0=mom_sb[:, tile, :], scalar=DECAY, in1=acc[tile][:], op0=MULT, op1=ADD
            )
            for first, n in STORES:
                if first + n - 1 == tile:
                    g = group_of(tile)
                    i0 = first - GROUPS[g][0]
                    nc.sync.dma_start(out=group_rows(out, g)[:, i0 : i0 + n, :], in_=mom_sb[:, first : first + n, :])

        vcopy, scopy = nc.vector.tensor_copy, nc.scalar.copy

        load_narrow(0, CHUNKS)
        load_wide(0, 2)
        load_wide(2, 2)
        for s in range(last):
            if s % CHUNKS == 0:
                for c in range(s, min(s + CHUNKS, last)):
                    cast_narrow(scopy, c)
                    quantise_narrow(c)
            if s == 2:
                load_narrow(CHUNKS, CHUNKS - 1)
                load_wide(CHUNKS, 2)
            if s == CHUNKS:
                load_wide(last - 1, 1)
                load_wide(last, 1)
                load_narrow(last, 1)
                for g, (first, n) in enumerate(GROUPS):
                    nc.sync.dma_start(out=mom_sb[:, first : first + n, :], in_=group_rows(mom, g))
            cast_wide(scopy, s, 1)
            cast_wide(vcopy, s, 0)
            cast_wide(vcopy, s, 2)
            quantise_wide(s, 0)
            quantise_wide(s, 2)
            if s < last - 1:
                multiply_group(s, 0)
            if s < last - 1:
                quantise_wide(s, 1)
            if s < last - 2:
                multiply_group(s, 1)

        quantise_wide(last - 1, 1, 0, 2)
        for tile in (4, 5):
            multiply(last - 1, tile)
        multiply_group(last - 2, 1)
        for tile in (0, 1):
            multiply(last - 1, tile)
        cast_wide_tiles(scopy, last, 1, 0, 2)
        cast_wide(vcopy, last, 0)
        quantise_wide(last - 1, 1, 2, 4)
        for tile in (6, 7, 2, 3):
            multiply(last - 1, tile)
        quantise_wide(last, 0)
        cast_narrow(vcopy, last, 0, LAST_SPLIT[0])
        cast_narrow(vcopy, last, LAST_SPLIT[0], LAST_SPLIT[1])
        cast_narrow(scopy, last, LAST_SPLIT[1], H)
        cast_wide_tiles(scopy, last, 1, 2, 4)
        cast_wide(scopy, last, 2)
        quantise_narrow(last, 0, H // 2)
        quantise_narrow(last, H // 2, H)
        quantise_wide(last, 1, 0, 2)
        for tile in range(6):
            multiply(last, tile)
        update(0)
        quantise_wide(last, 1, 2, 4)
        for tile in (6, 7):
            multiply(last, tile)
        update(1)
        quantise_wide(last, 2)
        for tile in range(BANKS, TILES):
            for s in range(PASSES):
                multiply(s, tile)
        for tile in range(2, TILES):
            update(tile)
